import numpy as np, ml_dtypes
CORES = [2,3,42,43,82,83,122,123]
N = 8
BF = ml_dtypes.bfloat16
def f(rng, *shape):
    return (rng.standard_normal(shape, dtype=np.float32) * np.exp2(rng.integers(-2, 3, shape[:-1] + (1,)))).astype(BF)
def wide(rng, *shape):
    v = f(rng, *shape).astype(np.float32); k = shape[:-2] + (1, shape[-1])
    return (v * np.exp2(rng.integers(-6, 7, k)) * (rng.random(k) > 0.0625)).astype(BF)
def entries(a):
    return np.ascontiguousarray(a.T).reshape(-1)
def table(e):
    return np.ascontiguousarray(np.reshape(e, (-1, 16)).T).astype(np.int32)
def gentries(a):
    return np.ascontiguousarray(a.reshape(8, 16, -1).transpose(0, 2, 1)).reshape(8, -1)
def gtable(e):
    e = np.asarray(e); return np.ascontiguousarray(e.reshape(8, -1, 16).transpose(0, 2, 1)).reshape(128, -1).astype(np.int32)
C, S, STEPS, X, NB = 3072, 48, 4, 7, 192
def others(r):
    a = np.arange(N * S); return a[a // S != r]
def field(v):
    return np.clip(v.astype(np.float32), -16, 16).astype(BF)
def draw(rng, every=False):
    s = rng.integers(0, C, (N, 8, C)); sd = np.zeros((N, N, S), np.int64); inner = []
    for r in range(N):
        p = rng.permutation(C); nb = NB
        if every:
            nb = N * S; p = p[(p > 0) & (p < C - 1)]; e = p[:nb - 2]; p = np.concatenate([[0, C - 1], p])
            sd[r] = np.roll(np.concatenate([[0], e[:2 * S - 2], [C - 1], e[2 * S - 2:]]).reshape(N, S), r + 1, axis=0)
        else:
            sd[r] = np.stack([rng.permutation(p[:nb])[:S] for q in range(N)])
        inner.append(p[nb:])
        s[r][rng.random((8, C)) < 0.125] = -1
        o = others(r)
        for g in range(8): s[r, g, rng.permutation(p[nb:])[:len(o)]] = C + rng.permutation(o)
    return s, sd, inner
def pack(rng, s, sd):
    m = [(rng.standard_normal((128, 128)) * 128 ** -0.5 * z).clip(-1, 1).astype(BF) for z in (0.85, 1.0)]
    return {"flow": field(f(rng, N, 128, C).astype(np.float32) * np.float32(0.5)), "mix": np.stack([m[0]] * N), "bend": np.stack([m[1]] * N),
            "links": np.stack([gtable(s[r]) for r in range(N)]), "sends": np.stack([table(sd[r].reshape(-1)) for r in range(N)])}
def setup_inputs(rng):
    s, sd, inner = draw(rng); return pack(rng, s, sd)
def setup_inputs_walls(rng):
    s, sd, inner = draw(rng, True)
    for r in range(N):
        o = rng.permutation(8); s[r][:, rng.permutation(C)[:256]] = -1; s[r][:, [0, C - 1]] = -1
        s[r, o[0]] = -1; s[r, o[1]] = np.where(s[r, o[1]] < 0, np.arange(C), s[r, o[1]])
    return pack(rng, s, sd)
def setup_inputs_repeats(rng):
    s, sd, inner = draw(rng)
    for r in range(N):
        o = rng.permutation(8); c = rng.integers(0, C, 8); c[o[0]] = 0; c[o[1]] = C - 1; e = others(r)
        near = (s[r] >= 0) & (s[r] < C) & (rng.random((8, C)) < 0.75)
        s[r] = np.where(near, c[:, None], s[r])
        s[r, o[2]] = np.where(s[r, o[2]] >= C, C + e[-1], s[r, o[2]]); s[r, o[3]] = np.where(s[r, o[3]] >= C, C + e[0], s[r, o[3]])
        sd[r, (r + 1) % N] = sd[r, (r + 1) % N, 0]
    return pack(rng, s, sd)
def setup_inputs_far(rng):
    s, sd, inner = draw(rng)
    for r in range(N):
        e = others(r); k = inner[r]; s[r][:, k] = C + rng.choice(e, (8, len(k)))
        s[r][:, k[0]] = C + e[0]; s[r][:, k[1]] = C + e[-1]
    return pack(rng, s, sd)
def setup_inputs_spread(rng):
    d = setup_inputs(rng); d["flow"] = field(wide(rng, N, 128, C).astype(np.float32) * np.float32(2.0 ** -7)); return d
def check_inputs(d):
    bad = []
    for a, b in (("flow", 16), ("mix", 1), ("bend", 1)):
        x = d[a].astype(np.float64)
        if not (np.abs(x) <= b).all(): bad.append(a + ": size")
        if a != "flow" and not (x == x[:1]).all(): bad.append(a + ": not alike on all ranks")
    s = np.stack([gentries(d["links"][r]) for r in range(N)]).astype(np.int64); sd = np.stack([entries(d["sends"][r]) for r in range(N)]).astype(np.int64)
    if (s < -1).any() or (s >= C + N * S).any(): bad.append("links: range")
    if (sd < 0).any() or (sd >= C).any(): bad.append("sends: range")
    if bad: return bad
    for r in range(N):
        if ((s[r] >= C) & ((s[r] - C) // S == r)).any(): bad.append("links: own rank's arrivals")
        if (s[r][:, sd[r]] >= C).any(): bad.append("a cell that is sent takes from another rank")
    if not bad:
        with np.errstate(all="ignore"): v, top = run(**d)
        if not (top <= 1024): bad.append("h or v of a step: size")
    return bad
def run(flow, mix, bend, links, sends):
    v = flow.astype(np.float64); m = mix.astype(np.float64); b = bend.astype(np.float64); top = 0.0
    s = np.stack([gentries(links[r]) for r in range(N)]).astype(np.int64)[:, :, None, :]
    sd = np.stack([entries(sends[r]).reshape(N, S) for r in range(N)]).astype(np.int64)
    opp = np.arange(8) ^ X
    for t in range(STEPS):
        h = np.stack([m[r].T @ v[r] + 0.125 * (b[r].T @ v[r]) ** 2 for r in range(N)])
        top = np.maximum(top, np.max(np.abs(h)))
        new = []
        for r in range(N):
            w = np.concatenate([h[r]] + [h[q][:, sd[q, r]] for q in range(N)], axis=1).reshape(8, 16, C + N * S)
            got = np.take_along_axis(w, np.maximum(s[r], 0), axis=2)
            new.append(np.where(s[r] < 0, h[r].reshape(8, 16, C)[opp], got).reshape(128, C))
        v = np.stack(new)
    return v, top
def reference(flow, mix, bend, links, sends):
    v, top = run(flow, mix, bend, links, sends)
    return {"y": v.astype(np.float32)}

from concourse.bass import DstId, RemoteDMATransfer
from concourse.mybir import AluOpType as Alu, ActivationFunctionType as Act

N, C, S, STEPS = 8, 3072, 48, 4
NS = (N - 1) * S
KS = NS // 16
H0, AR, PH = NS, NS + C, NS + C + N * S
WIN = PH + C
WALL = C + N * S
SLOT = [0, 1, 2, 3, 7, 6, 5, 4]
SENT = [96, 240]
MAIN = [384, 512, 512, 512, 512, 448, 128, 64]
FLOW = [(0, 896), (896, 1920), (1920, 3072)]
OUT = [(0, 320), (320, 960), (960, 1728), (1728, 2432), (2432, 3072)]
ROOT8 = 0.125 ** 0.5
DMA_SEMS = ["d%d" % k for k in range(32)]

SCRATCH = {
    "fl": ("sbuf", [128, C], "bfloat16"), "fs": ("sbuf", [128, NS], "bfloat16"),
    "wn": ("sbuf", [128, 2, 128], "bfloat16"), "w1": ("sbuf", [128, 2, 128], "bfloat16"),
    "w2": ("sbuf", [128, 2, 128], "bfloat16"), "w4": ("sbuf", [128, 2, 128], "bfloat16"),
    "hi": ("sbuf", [128, NS + C], "bfloat16"), "mid": ("sbuf", [128, NS + C], "bfloat16"),
    "lo": ("sbuf", [128, NS + C], "bfloat16"), "rest": ("sbuf", [128, NS + C], "float32"),
    "sq": ("sbuf", [128, NS + C], "float32"), "yb": ("sbuf", [128, C], "float32"),
    "lk": ("sbuf", [128, 192], "int32"), "la": ("sbuf", [128, 192], "int32"), "w0": ("sbuf", [128, 192], "int32"),
    "wt": ("sbuf", [128, 192], "float32"), "lm": ("sbuf", [128, 192], "float32"), "lf": ("sbuf", [128, 192], "float32"),
    "ln16": ("sbuf", [128, 192], "uint16"), "ls16": ("sbuf", [128, 192], "uint16"),
    "sd": ("sbuf", [128, 24], "int32"), "sf": ("sbuf", [128, 24], "float32"), "si": ("sbuf", [128, 24], "int32"),
    "sa": ("sbuf", [128, 24], "int32"), "sb": ("sbuf", [128, 24], "int32"),
    "s16": ("sbuf", [128, 24], "uint16"), "sa16": ("sbuf", [128, 24], "uint16"), "sb16": ("sbuf", [128, 24], "uint16"),
    "c16": ("sbuf", [128, 24], "uint16"), "c1": ("sbuf", [128, 24], "float32"), "c2": ("sbuf", [128, 24], "float32"),
    "c3": ("sbuf", [128, 24], "float32"), "jt": ("sbuf", [128, 24], "float32"), "pm": ("sbuf", [128, 4], "float32"),
    "i1": ("sbuf", [128, NS], "int32"), "a1": ("sbuf", [128, NS], "int32"),
    "dg": ("sbuf", [128, NS], "float32"), "nd": ("sbuf", [128, NS], "float32"), "mk": ("sbuf", [128, NS], "float32"),
    "wh": ("sbuf", [128, NS], "float16"), "xd": ("sbuf", [128, NS], "float32"), "yd": ("sbuf", [128, NS], "float32"),
    "ones": ("sbuf", [128, 128], "float32"), "ps": ("sbuf", [128, 128], "float32"),
    "po": ("sbuf", [128, 128], "float32"), "b1": ("sbuf", [128, 128], "float32"), "b2": ("sbuf", [128, 128], "float32"),
    "bh": ("sbuf", [128, 128], "float16"),
}
for _t in range(STEPS):
    SCRATCH["win%d" % _t] = ("sbuf", [128, WIN], "float32")
    SCRATCH["hs%d" % _t] = ("sbuf", [128, NS], "float32")
for _b in range(8):
    SCRATCH["bank%d" % _b] = ("psum", [128, 512], "float32")

SEMAPHORES = ["pe", "act", "dve", "pool", "sent"] + ["arr%d" % t for t in range(STEPS)] + DMA_SEMS

ORDER_1 = {
    "pe": "LP B2.0 SR M2.0 M3.0 B0.0 M0.0 B1.0 M1.0 M4.0 B4.0 B3.0 B6.0 U B5.0 M6.0 M5.0 B8.0 M9.0 B7.0 M8.0 M7.0 B9.0",
    "act": "ldlk ldbend w1b w1a w1e w1d w1c sq2.0 fs0 fs1 sq0.0 sq1.0 mk sq4.0 sq3.0 sq6.0 sq5.0 hsb sq8.0 sq7.0 sq9.0",
    "dve": "own3 ones a1 pm wt la lm dg sf0 sf1 sf2 sf3 jt nd lf bh s16 si ls16 sb sa add2.0 sa16 add0.0 own2 sb16 own1 "
           "add1.0 own0 hsa wh add4.0 ln16 add3.0 xd yd add5.0 c1 add6.0 c2 add8.0 c3 add7.0 add9.0 c16",
    "sp": "ldmix ldfl0 ldsd ldfl2 ldfl1 w2 swap0.0 swap1.0 swap2.0 swap3.0 w4",
    "pool": "i1 w0 psa psb b1 b2 send0.0 send1.0 po",
}
ORDER_2 = {
    "pe": "Bh1 Mh0 Bh0 Mh1 Mm0 Bm0 Mm1 Bm1 Ml0 Bl0 Bl1 Ml1 Bh2 Mh2 Bh3 Mh3 Bm2 Mm2 Mh4 Ml2 Mm3 Bl2 Bh4 Bm3 Ml3 Bm4 Bl3 Mm4 "
          "Bl4 Bh5 Ml4 Bm5 Mh5 Bl5 Mm5 Ml5 Bh6 Mh6 Mh7 Bh9 Mm6 Bh7 Mm7 Bm6 Bm7 Bl6 Ml6 Mh8 Bl7 Bm9 Bh8 Bl9 Ml7 Bm8 Bl8 "
          "Mh9 Mm9 Mm8 Ml9 Ml8",
    "act": "hi0 mid0 hi2 hi3 mid2 sq0 hi4 mid3 sq1 hi5 mid4 hi7 hi6 mid5 hi8 sq2 sq4 sq3 sq5 mid6 mid7 hi9 mid9 sq6 sq7 sq9 sq8",
    "dve": "hi1 r0 r1 mid1 lo0 lo1 r2 r3 add0 lo2 r4 add1 lo3 r5 lo4 r7 lo5 r6 add2 add4 add3 add5 r8 r9 lo6 mid8 lo8 lo7 "
           "lo9 add6 add7 add9 add8",
}
ORDER_34 = {
    "pe": "Bh0 Mh0 Bh1 Mh1 Bh2 Mh2 Bm0 Mm0 Bl0 Ml0 Mm1 Bm1 Bh3 Mh3 Bl1 Mm2 Ml1 Mh4 Bm2 Bh4 Bl2 Ml2 Bm3 Mm3 Bh5 Mh5 Bl3 Ml3 "
          "Bm4 Bl4 Mm4 Ml4 Bm5 Bl5 Mm5 Ml5 Bh6 Bm6 Bl6 Mh6 Mm6 Ml6 Bh7 Bm7 Mh7 Mm7 Bl7 Mh8 Ml7 Bh8 Bm8 Bl8 Bh9 Bm9 Bl9 "
          "Mm8 Ml8 Mh9 Mm9 Ml9",
    "act": "hi0 hi2 mid0 mid1 hi3 sq0 mid2 hi4 sq1 mid3 hi5 sq2 mid4 mid5 hi6 sq3 sq4 mid6 hi8 sq5 hi7 hi9 mid7 mid8 sq6 "
           "sq7 sq8 sq9",
    "dve": "hi1 r0 r1 lo0 r2 lo1 r3 add0 lo2 add1 r4 lo3 r5 lo4 lo5 r6 add3 add2 add4 lo6 add5 r7 r8 r9 lo7 add6 mid9 "
           "lo8 lo9 add7 add8 add9",
}
ORDER_END = {
    "act": "ya0 ya1 ya2 cp0 ya3 ya4",
    "dve": "yb0 yb1 yb2 yb3 cp1 yb4",
    "pe": "P0 P1",
    "sp": "st0 st1 st2 st3 st4",
}


def calls_of(rank, cores, topo):
    me = cores[rank]
    order = [(rank + k) % N for k in range(1, N)]
    near = [q for q in order if topo.chip(cores[q]) == topo.chip(me)]
    far = [q for q in order if q not in near]
    chips = []
    for q in far:
        if topo.chip(cores[q]) not in chips:
            chips.append(topo.chip(cores[q]))
    chips.sort(key=lambda ch: topo.same_plane(topo.chip(me), ch))
    far = [q for ch in chips for q in sorted(far) if topo.chip(cores[q]) == ch]
    out = [e for e in topo.engines(me, cores[far[0]]) if all(e in topo.engines(me, cores[q]) for q in far)]
    calls = []
    for part in (far[:SENT[0] // S], far[SENT[0] // S:]):
        n = len(out) // len(part)
        calls.append([(q, out[i * n:(i + 1) * n]) for i, q in enumerate(part)])
    for q in near:
        own = [e for e in topo.engines(me, cores[q]) if e not in out]
        calls[1].append((q, own[:len(calls[1][0][1])]))
    for call in calls:
        for q, _ in call:
            assert topo.may_write(me, cores[q])
    return calls


def rank_program(g, core, T, topo):
    rank = T.rank_of(core)
    if rank is None:
        return
    V, A, PE, SP = g.vector, g.scalar, g.tensor, g.sync
    queue = {"pe": PE, "act": A, "dve": V, "sp": SP, "pool": g}
    calls = calls_of(rank, T.cores, topo)
    peers = [q for call in calls for q, _ in call]
    ops, made, orders = {}, [], {q: [] for q in queue}
    free_sems = list(DMA_SEMS)

    def op(name, fn, reads, writes, after=(), dma=0, fixed=None):
        deps = list(after)
        writes = list(writes) + [x for x in reads if x[0].startswith("bank")]
        for other in made:
            o = ops[other]
            for mine, theirs in ((reads, o["w"]), (writes, o["w"]), (writes, o["r"])):
                if any(a[0] == b[0] and a[1] < b[2] and b[1] < a[2] for a in mine for b in theirs):
                    deps.append(other)
                    break
        ops[name] = {"fn": fn, "r": reads, "w": writes, "deps": deps, "dma": dma, "token": fixed, "clock": {}}
        made.append(name)

    def whole(*names):
        return [(n, 0, 1 << 20) for n in names]

    def dmas(pairs):
        def fn(q, sem):
            for out, in_ in pairs:
                q.dma_start(out, in_).then_inc(sem, 16)
        return fn

    def dma(name, pairs, reads, writes, after=()):
        op(name, dmas(pairs), reads, writes, after, dma=len(pairs))

    def copy(q, out, in_):
        return V.tensor_copy(out, in_) if q is V else A.activation(out, in_, Act.Copy)

    def ts(out, in0, s1, op0, s2=None, op1=None):
        if op1 is None:
            return lambda q: V.tensor_scalar(out, in0, s1, None, op0)
        return lambda q: V.tensor_scalar(out, in0, s1, s2, op0, op1)

    def tt(out, in0, in1, alu):
        return lambda q: V.tensor_tensor(out, in0, in1, alu)

    def cp(out, in_):
        return lambda q: copy(q, out, in_)

    def mm(out, lhsT, rhs, start=True, stop=True):
        return lambda q: PE.matmul(out, lhsT, rhs, start, stop)

    bank = [T["bank%d" % b] for b in range(8)]
    win = [T["win%d" % t] for t in range(STEPS)]
    hs = [T["hs%d" % t] for t in range(STEPS)]

    dma("ldmix", [(T.wn[:, 0, :], T.mix[:])], [], [("wn", 0, 128)])
    dma("ldbend", [(T.wn[:, 1, :], T.bend[:])], [], [("wn", 128, 256)])
    dma("ldlk", [(T.lk[:], T.links[:])], [], whole("lk"))
    dma("ldsd", [(T.sd[0:16, :], T.sends[:])], [], whole("sd"))
    for k, (a, b) in enumerate(FLOW):
        dma("ldfl%d" % k, [(T.fl[:, a:b], T.flow[:, a:b])], [], [("fl", a, b)])

    op("ones", lambda q: V.memset(T.ones[:], 1.0), [], whole("ones"))
    for t in range(STEPS):
        a = AR + rank * S
        op("own%d" % t, lambda q, t=t, a=a: V.memset(win[t][:, a:a + S], 0.0), [], [("win%d" % t, a, a + S)])
        total = sum(len(e) for src in range(N) if src != rank for call in calls_of(src, T.cores, topo) for q, e in call if q == rank)
        op("arr%d" % t, None, [], [("win%d" % t, AR, a), ("win%d" % t, a + S, PH)], fixed=("arr%d" % t, total))
    op("i1", lambda q: g.iota(T.i1[:], [[0, KS], [-1, 16]], 16, 1), [], whole("i1"))
    op("w0", lambda q: g.iota(T.w0[:], [[16, 192]], WALL, 0), [], whole("w0"))
    op("a1", ts(T.a1[:], T.i1[:], 15, Alu.bitwise_and), whole("i1"), whole("a1"))
    op("pm", cp(T.pm[:, 0:1], T.a1[:, 0:1]), whole("a1"), whole("pm"))
    op("wt", ts(T.wt[:], T.w0[:], T.pm[:, 0:1], Alu.add), whole("w0", "pm"), whole("wt"))
    op("dg", ts(T.dg[:], T.a1[:], 0.0, Alu.is_equal), whole("a1"), whole("dg"))
    op("nd", ts(T.nd[:], T.a1[:], 0.0, Alu.not_equal), whole("a1"), whole("nd"))
    op("jt", ts(T.jt[:, 0:KS], T.wt[:, 0:KS], -float(WALL + NS + 1024), Alu.add), whole("wt"), whole("jt"))
    op("psa", lambda q: g.affine_select(T.ps[:, 0:64], T.ones[:, 0:64], [[-1, 64]], Alu.is_equal, 0.0, 0, 1),
       whole("ones"), [("ps", 0, 64)])
    op("psb", lambda q: g.affine_select(T.ps[:, 64:128], T.ones[:, 0:64], [[16, 4], [-1, 16]], Alu.is_equal, 0.0, -112, 1),
       whole("ones"), [("ps", 64, 128)])
    op("po", lambda q: g.affine_select(T.po[:], T.ones[:], [[16, 8], [-1, 16]], Alu.is_equal, 0.0, -112, 1),
       whole("ones"), whole("po"))
    op("b1", lambda q: g.affine_select(T.b1[:], T.ones[:], [[-16, 8], [0, 16]], Alu.is_ge, 0.0, 0, 1), whole("ones"), whole("b1"))
    op("b2", lambda q: g.affine_select(T.b2[:], T.b1[:], [[16, 8], [0, 16]], Alu.is_ge, 0.0, 15, -1), whole("b1"), whole("b2"))
    op("bh", cp(T.bh[:], T.b2[:]), whole("b2"), whole("bh"))

    op("w1a", cp(T.w1[:, :, 0:64], T.wn[:, :, 0:64]), whole("wn"), [("w1", 0, 64)])
    for s, name in zip(range(4, 8), "bcde"):
        d = SLOT[s]
        op("w1" + name, cp(T.w1[:, :, 16 * s:16 * s + 16], T.wn[:, :, 16 * d:16 * d + 16]), whole("wn"), [("w1", 16 * s, 16 * s + 16)])
    slots = [(0, 0, 64)] + [(16 * s, 16 * SLOT[s], 16) for s in range(4, 8)]
    dma("w2", [(T.w2[p:p + n], T.w1[o:o + n]) for p, o, n in slots], whole("w1"), whole("w2"))
    dma("w4", [(T.w4[p:p + n], T.wn[o:o + n]) for p, o, n in slots], whole("wn"), whole("w4"))

    op("la", ts(T.la[:], T.lk[:], 8191, Alu.bitwise_and), whole("lk"), whole("la"))
    op("lm", tt(T.lm[:], T.la[:], T.wt[:], Alu.min), whole("la", "wt"), whole("lm"))
    op("ln16", cp(T.ln16[:], T.lm[:]), whole("lm"), whole("ln16"))
    op("LP", mm(bank[6][:, 0:192], T.ps[:], T.lm[:]), whole("ps", "lm"), whole("bank6"))
    op("lf", ts(T.lf[:], bank[6][:, 0:192], float(C), Alu.min, -1024.0, Alu.add), whole("bank6"), whole("lf"))
    op("ls16", cp(T.ls16[:], bank[6][:, 0:192]), whole("bank6"), whole("ls16"))
    runs = []
    for j, q in enumerate(peers):
        if runs and runs[-1][1] + runs[-1][2] == 3 * q and runs[-1][2] < 6:
            runs[-1][2] += 3
        else:
            runs.append([3 * j, 3 * q, 3])
    assert len(runs) == 4
    for k, (a, b, n) in enumerate(runs):
        op("sf%d" % k, cp(T.sf[0:16, a:a + n], T.sd[0:16, b:b + n]), whole("sd"), [("sf", a, a + n)])
    op("SR", mm(bank[7][:, 0:KS], T.dg[0:16, 0:128], T.sf[0:16, 0:KS]), whole("dg", "sf"), whole("bank7"))
    op("s16", cp(T.s16[:, 0:KS], bank[7][:, 0:KS]), whole("bank7"), whole("s16"))
    op("si", cp(T.si[:, 0:KS], bank[7][:, 0:KS]), whole("bank7"), whole("si"))
    op("sa", ts(T.sa[:, 0:KS], T.si[:, 0:KS], 4, Alu.arith_shift_right), whole("si"), whole("sa"))
    op("sb", ts(T.sb[:, 0:KS], T.si[:, 0:KS], 15, Alu.bitwise_and), whole("si"), whole("sb"))
    op("sa16", cp(T.sa16[:, 0:KS], T.sa[:, 0:KS]), whole("sa"), whole("sa16"))
    op("sb16", cp(T.sb16[:, 0:KS], T.sb[:, 0:KS]), whole("sb"), whole("sb16"))
    op("mk", cp(T.mk[:], T.dg[:, 0:16].indirect(T.sb16[:, 0:KS])), whole("dg", "sb16"), whole("mk"))
    op("wh", tt(T.wh[:], T.lf[:, 0:192].indirect(T.sa16[:, 0:KS]), T.mk[:], Alu.mult), whole("lf", "sa16", "mk"), whole("wh"))

    blocks, at = [], 0
    for n in SENT + MAIN:
        blocks.append((at, at + n))
        at += n
    pair = [0]

    def collide(t, k, parts, weights):
        a, b = blocks[k]
        n = b - a
        bb, bm = 2 * (pair[0] % 4), 2 * (pair[0] % 4) + 1
        pair[0] += 1
        for m, bk, w, wr in (("B", bb, weights[1], weights[2]), ("M", bm, weights[0], weights[2])):
            for i, (tag, ap, region) in enumerate(parts):
                op("%s%s%d.%d" % (m, tag, k, t), mm(bank[bk][:, 0:n], w, ap, i == 0, i == len(parts) - 1),
                   [region] + whole(wr), whole("bank%d" % bk))
        op("sq%d.%d" % (k, t), lambda q: A.activation(T.sq[:, a:b], bank[bb][:, 0:n], Act.Square, scale=ROOT8),
           whole("bank%d" % bb), [("sq", a, b)])
        out, region = (hs[t][:, a:b], ("hs%d" % t, a, b)) if a < NS else (win[t][:, a:b], ("win%d" % t, a, b))
        op("add%d.%d" % (k, t), tt(out, bank[bm][:, 0:n], T.sq[:, a:b], Alu.add), whole("bank%d" % bm) + [("sq", a, b)], [region])

    def send(t, k):
        a, b = blocks[k]

        def fn(q):
            trs = []
            for j, (dst, engines) in enumerate(calls[k]):
                rid, pid, _ = topo.addr(T.cores[dst])
                trs.append(RemoteDMATransfer(dst_ids=[DstId(rid=rid, pnc=pid)], dma_engine_mask=sum(1 << e for e in engines),
                                             remote_sem=T.sem["arr%d" % t], src=hs[t][:, a + j * S:a + (j + 1) * S],
                                             dst=win[t][:, AR + rank * S:AR + (rank + 1) * S]))
            g.remote_dma_fused(trs, local_sem=T.sem.sent)
        op("send%d.%d" % (k, t), fn, [("hs%d" % t, a, b)], [], dma=-sum(len(e) for _, e in calls[k]))

    def swap(name, t, a, b, groups, after=()):
        w = win[t]
        dma(name, [(w[p:p + n, PH + a:PH + b], w[o:o + n, H0 + a:H0 + b]) for p, o, n in groups],
            [("win%d" % t, H0 + a, H0 + b)], [("win%d" % t, PH + a, PH + b)] if groups[0][0] == 0 else [(name, 0, 1)], after)

    halves = [(0, 64, 64), (64, 0, 64)]
    groups = [(16 * d, 16 * (7 - d), 16) for d in range(8)]

    w1 = (T.w1[:, 0, :], T.w1[:, 1, :], "w1")
    for k in (2, 3, 0, 1):
        a, b = blocks[k]
        if k < 2:
            op("fs%d" % k, cp(T.fs[:, a:b], T.fl[:, 0:C].indirect(T.s16[:, a // 16:b // 16])), whole("fl", "s16"), [("fs", a, b)])
            collide(0, k, [("", T.fs[:, a:b], ("fs", a, b))], w1)
            send(0, k)
        else:
            collide(0, k, [("", T.fl[:, a - NS:b - NS], ("fl", a - NS, b - NS))], w1)
    op("U", mm(bank[4][:, 0:NS], T.bh[:], T.wh[:]), whole("bh", "wh"), whole("bank4"))
    op("xd", tt(T.xd[:], bank[4][:, 0:NS], T.dg[:], Alu.mult), whole("bank4", "dg"), whole("xd"))
    op("yd", lambda q: V.tensor_tensor_scan(T.yd[:], T.nd[:], T.xd[:], 0.0, Alu.mult, Alu.add), whole("nd", "xd"), whole("yd"))
    op("c1", ts(T.c1[:, 0:KS], T.yd[:, 15:NS:16], C - 1024.5, Alu.is_ge, -8192.0, Alu.mult), whole("yd"), whole("c1"))
    op("c2", tt(T.c2[:, 0:KS], T.yd[:, 15:NS:16], T.c1[:, 0:KS], Alu.add), whole("yd", "c1"), whole("c2"))
    op("c3", tt(T.c3[:, 0:KS], T.c2[:, 0:KS], T.jt[:, 0:KS], Alu.max), whole("c2", "jt"), whole("c3"))
    op("c16", ts(T.c16[:, 0:KS], T.c3[:, 0:KS], float(NS + 1024), Alu.add), whole("c3"), whole("c16"))
    op("hsa", cp(win[0][0:64, 0:NS], hs[0][64:128, :]), whole("hs0"), [("win0", 0, NS)])
    op("hsb", cp(win[0][64:128, 0:NS], hs[0][0:64, :]), whole("hs0"), [("hsb", 0, 1)])
    for k in range(4, 10):
        if k == 6:
            pair[0] += 1
        a, b = blocks[k]
        collide(0, k, [("", T.fl[:, a - NS:b - NS], ("fl", a - NS, b - NS))], w1)
    cuts = [0, 384, 896, 1920, C]
    for i in range(4):
        swap("swap%d.0" % i, 0, cuts[i], cuts[i + 1], halves, after=["add5.0"] if i == 2 else [])
    for q in ORDER_1:
        orders[q] += ORDER_1[q].split()

    for t in range(1, STEPS):
        last = t == STEPS - 1
        w = T.w4 if last else T.w2
        weights = (w[:, 0, :], w[:, 1, :], "w4" if last else "w2")
        for k, (a, b) in enumerate(blocks):
            if k < 2:
                src = win[t - 1][:, 0:AR].indirect(T.c16[:, a // 16:b // 16])
                reads = [("win%d" % (t - 1), 0, AR)] + whole("c16", "hsb")
            else:
                end = PH + min(c for c in cuts if c >= b - NS)
                src = win[t - 1][:, H0:end].indirect(T.ls16[:, (a - NS) // 16:(b - NS) // 16])
                reads = [("win%d" % (t - 1), H0, end)] + whole("ls16")
            tag = "%d.%d" % (k, t)
            op("hi" + tag, cp(T.hi[:, a:b], src), reads, [("hi", a, b)])
            op("r" + tag, tt(T.rest[:, a:b], src, T.hi[:, a:b], Alu.subtract), reads + [("hi", a, b)], [("rest", a, b)])
            op("mid" + tag, cp(T.mid[:, a:b], T.rest[:, a:b]), [("rest", a, b)], [("mid", a, b)])
            op("lo" + tag, tt(T.lo[:, a:b], T.rest[:, a:b], T.mid[:, a:b], Alu.subtract), [("rest", a, b), ("mid", a, b)], [("lo", a, b)])
            collide(t, k, [(x[0], T[x][:, a:b], (x, a, b)) for x in ("hi", "mid", "lo")], weights)
            if k < 2:
                send(t, k)
        order = ORDER_2 if t == 1 else ORDER_34
        for q in order:
            orders[q] += ["%s.%d" % (x, t) for x in order[q].split()]
        orders["pool"] += ["send0.%d" % t, "send1.%d" % t]
        if not last:
            cuts = [0, 1920, C]
            dma("swaps.%d" % t, [(win[t][p:p + n, 0:NS], hs[t][o:o + n, :]) for p, o, n in halves],
                whole("hs%d" % t), [("win%d" % t, 0, NS)])
            swap("swap0.%d" % t, t, cuts[0], cuts[1], halves)
            swap("swap1.%d" % t, t, cuts[1], cuts[2], halves)
            orders["sp"] += ["swaps.%d" % t, "swap0.%d" % t, "swap1.%d" % t]

    t = STEPS - 1
    cuts = [0, 1408, 2432, C]
    swap("swap0.3", t, cuts[0], cuts[1], groups)
    swap("swap1.3", t, cuts[1], cuts[2], groups[:5])
    swap("swap2.3", t, cuts[1], cuts[2], groups[5:])
    orders["sp"] += ["swap0.3", "swap1.3"]
    orders["act"].insert(orders["act"].index("sq7.3"), "swap2.3")
    for i, (a, b) in enumerate(((2432, 2880), (2880, C))):
        bk = 2 * (pair[0] % 4) + i
        op("P%d" % i, mm(bank[bk][:, 0:b - a], T.po[:], win[t][:, H0 + a:H0 + b]), whole("po") + [("win3", H0 + a, H0 + b)],
           whole("bank%d" % bk))
        op("cp%d" % i, cp(win[t][:, PH + a:PH + b], bank[bk][:, 0:b - a]), whole("bank%d" % bk), [("win3", PH + a, PH + b)])
    for i, (a, b) in enumerate(OUT):
        end = min(c for c in cuts if c >= b)
        half = (a + b) // 2
        for tag, c, d in (("ya", a, half), ("yb", half, b)):
            op("%s%d" % (tag, i), cp(T.yb[:, c:d], win[t][:, H0:PH + end].indirect(T.ln16[:, c // 16:d // 16])),
               [("win3", H0, PH + end)] + whole("ln16") + (whole("swap2.3") if end > cuts[1] else []), [("yb", c, d)])
        dma("st%d" % i, [(T.y[:, a:b], T.yb[:, a:b])], [("yb", a, b)], [])
    for q in ORDER_END:
        orders[q] += ORDER_END[q].split()

    where = {name: q for q in orders for name in orders[q]}
    assert sorted(where) == sorted(n for n in made if ops[n]["fn"] is not None), set(where) ^ set(made)
    count = {s: 0 for s in SEMAPHORES}
    waited = {s: 0 for s in SEMAPHORES}
    known = {q: {} for q in queue}
    at = {q: 0 for q in queue}
    for n in made:
        if ops[n]["fn"] is None:
            count[ops[n]["token"][0]] = ops[n]["token"][1]
    left = len(where)
    while left:
        before = left
        for q in queue:
            while at[q] < len(orders[q]):
                o = ops[orders[q][at[q]]]
                if any(ops[d]["token"] is None for d in o["deps"]):
                    break
                need = {}
                for d in o["deps"]:
                    if q == "pe" and where.get(d) == "pe":
                        continue
                    sem, val = ops[d]["token"]
                    if val > need.get(sem, (0, None))[0]:
                        need[sem] = (val, d)
                for sem in need:
                    val = need[sem][0]
                    if known[q].get(sem, 0) >= val or any(s != sem and ops[need[s][1]]["clock"].get(sem, 0) >= val for s in need):
                        continue
                    queue[q].wait_ge(T.sem[sem], val)
                    waited[sem] = max(waited[sem], val)
                for sem, (val, d) in need.items():
                    known[q][sem] = max(known[q].get(sem, 0), val)
                    for s, v in ops[d]["clock"].items():
                        known[q][s] = max(known[q].get(s, 0), v)
                if o["dma"] > 0:
                    sem = free_sems.pop(0)
                    o["fn"](queue[q], T.sem[sem])
                    count[sem] = 16 * o["dma"]
                elif o["dma"] < 0:
                    sem = "sent"
                    o["fn"](queue[q])
                    count[sem] -= o["dma"]
                else:
                    sem = q
                    o["fn"](queue[q]).then_inc(T.sem[sem], 1)
                    count[sem] += 1
                o["token"] = (sem, count[sem])
                o["clock"] = dict(known[q])
                at[q] += 1
                left -= 1
        assert left < before, [orders[q][at[q]] for q in queue if at[q] < len(orders[q])]
    for sem in SEMAPHORES:
        if count[sem] > waited[sem]:
            g.wait_ge(T.sem[sem], count[sem])
